import numpy as np, ml_dtypes
CORES = [40,64,80,88,96,104,120,144]
N = 8
import mx_ref
BF = ml_dtypes.bfloat16
def gcols(t, e):
    v = np.concatenate([t.reshape(8, 16, -1, 4), np.zeros((8, 16, 1, 4), BF)], axis=2)
    return np.ascontiguousarray(np.stack([v[g][:, e[g]] for g in range(8)])).reshape(128, -1)
def tile(rs):
    return np.stack(rs, axis=2).reshape(128, -1).astype(BF)
def pick(q, e):
    c = np.concatenate([q[0].reshape(128, -1, 4), np.zeros((128, 1, 4), np.uint8)], axis=1); s = np.concatenate([q[1], np.ones((16, 1), np.uint8)], axis=1)
    return (np.ascontiguousarray(c[:, e].reshape(128, -1)), np.ascontiguousarray(s[:, e]))
def join(*qs):
    return (np.concatenate([q[0] for q in qs], axis=1), np.concatenate([q[1] for q in qs], axis=1))
def put(q, e, v):
    c, s = q[0].reshape(128, -1, 4).copy(), q[1].copy(); c[:, e] = v[0].reshape(128, -1, 4); s[:, e] = v[1]
    return (c.reshape(128, -1), s)
def pk(c, s):
    return (np.ascontiguousarray(c), mx_ref.live(s))
def emit(q):
    return q[0], q[1]
def packed(v, rng):
    q = [mx_ref.quantize(np.ascontiguousarray(v[r])) for r in range(N)]
    return np.stack([a for a, b in q]), np.stack([mx_ref.plane(b, rng) for a, b in q])
def values_of_codes():
    e, c = np.zeros((128, 128, 4), np.float32), np.zeros((128, 2, 4), np.uint8)
    e[np.arange(128), np.arange(128), 0] = 1
    c[:127, :, 0] = np.arange(256).reshape(2, 128).T[:127]
    return mx_ref.matmul(mx_ref.quantize(e.reshape(128, 512).astype(BF)), (c.reshape(128, 8), np.full((16, 2), 127, np.uint8))).T.reshape(-1).astype(np.float64)
CODE_VALUE, SCALE_VALUE = values_of_codes(), 2.0 ** (np.arange(256) - 127.0)
def decode(q):
    return (CODE_VALUE[q[0]].reshape(16, 8, -1, 4) * SCALE_VALUE[q[1]][:, None, :, None] + 0.0).reshape(128, -1).astype(np.float32)
def f(rng, *shape):
    return mx_ref.flush((rng.standard_normal(shape, dtype=np.float32) * np.exp2(rng.integers(-2, 3, shape[:-1] + (1,)))).astype(BF))
def wide(rng, *shape, cols=0):
    v = rng.standard_normal(shape, dtype=np.float32) * np.exp2(rng.integers(-12, 13, shape)).astype(np.float32)
    if cols: v *= np.repeat(np.exp2(rng.integers(-cols, cols + 1, shape[:-2] + (1, shape[-1] // 4))) * (rng.random(shape[:-2] + (1, shape[-1] // 4)) > 0.0625), 4, axis=-1).astype(np.float32)
    return mx_ref.flush(v.astype(BF))
C, B = 448, 192
def big(v):
    v = v.astype(np.float32)
    v[np.abs(v) < np.float32(2.0 ** -16)] = 0
    return v.astype(BF)
def shared(u):
    u = np.array(u).reshape(8, 16, 8, 16, 4)
    for g in range(8): u[np.arange(8) != g, :, g, 0] = 0
    return np.repeat(u.reshape(1, 128, 512), N, axis=0)
def numbers_of(rng):
    return {"x": big(f(rng, N, 128, 4 * C)), "h": np.array(f(rng, N, 128, 4 * B)), "u": shared(f(rng, 128, 512)), "v": np.array(f(rng, N, 128, 512))}
def layers(rng, still=[]):
    w = np.array(f(rng, N, 128, 2048)).reshape(N, 8, 16, 4, 8, 16, 4)
    for i in still:
        w[:, :, i] = 0
        w[:, :, :, :, :, i] = 0
    return w
def weights(rng, w):
    c, p = packed(np.ascontiguousarray(w).reshape(N, 128, 2048), rng)
    return {"wc": c, "ws": p}
def tiles(x, h, u, v):
    return {"x": x.reshape(N, 128, 4 * C).astype(BF), "h": h.reshape(N, 128, 4 * B).astype(BF), "u": shared(u), "v": v}
def setup_inputs(rng):
    return {**numbers_of(rng), **weights(rng, layers(rng))}
def setup_inputs_ties(rng):
    d = numbers_of(rng)
    e = rng.permutation(N)
    a = (rng.integers(4, 8, (8, 8, 3, 4)) * rng.choice([-1.0, 1.0], (8, 8, 3, 4))).astype(np.float32).astype(BF)
    a[:, :, 2] = 0
    x, h = d["x"].reshape(N, 8, 16, C, 4), d["h"].reshape(N, 8, 16, B, 4)
    for r in range(N):
        for g in range(8):
            x[r, g, :8] = a[g][:, np.zeros(C, int) if r == e[0] else rng.permutation(C) % 3]
            h[r, g, :8] = a[g][:, rng.permutation(B) % 3]
    x[e[1]] = 0
    u = d["u"][0].copy().reshape(8, 16, 8, 16, 4)
    u[:, 8:, :, 0] = 0
    return {**tiles(x, h, u, d["v"]), **weights(rng, layers(rng, range(8)))}
def setup_inputs_near(rng):
    d = numbers_of(rng)
    a, c = rng.permutation(8), rng.permutation(8) % 2 * 2.0 - 1.0
    o = a % 4
    size = np.where(o == 3, 2.0 ** -6, 1.0)[:, None, None]
    x, h = d["x"].astype(np.float32).reshape(N, 8, 16, C, 4), d["h"].astype(np.float32).reshape(N, 8, 16, B, 4)
    shift = rng.integers(0, C, (N, 8, 1))
    for t, s in ((x, (np.arange(C) + shift) % C // 2), (h, np.argsort(rng.random((N, 8, B)), axis=2) * (C // 2) // (B - 1))):
        k = ((s[..., None] >> np.arange(8)) & 1) * np.exp2(np.arange(8) - 23.0) * size
        t[:, :, 0] = 0
        t[:, :, 0, :, 0] = np.where(o < 2, c, 0)[:, None]
        t[:, :, 8] = k[..., :4]
        t[:, :, 9] = k[..., 4:]
        t[:, :, 10:] = rng.integers(4, 8, (N, 8, 6, s.shape[2], 4)) * 2.0 ** -20 * size[..., None]
        t[:, :, 10, :, 0] = np.where(o < 2, 2.0 ** -16, 0)[:, None]
        t[:, :, 11, :, 0] = 2.0 ** -20 * size[..., 0]
    h[:, o == 3, 10, 1::2, 0] = 2.0 ** -30
    at = np.argsort(a)
    for r in range(N):
        for g in np.concatenate([rng.permutation(at[:4])[:2], rng.permutation(at[4:])[:2]]):
            x[r, g, 0, (C // 4 + rng.integers(C // 2) - shift[r, g, 0]) % C, 0] = rng.choice([-1.0, 1.0]) * 2.0 ** 30
    u = d["u"][0].astype(np.float32).reshape(128, 128, 4)
    u[:, ::16] = 0
    for g in range(8):
        k = 1.0 if o[g] == 0 else 2.0 ** -30
        u[16 * g, 16 * g, 0] = k
        u[16 * g + 8:16 * g + 10, 16 * g] = k
        u[16 * g + 10, 16 * g, 0] = k * (64.0 if o[g] < 2 else 1.0)
        u[16 * g + 11, 16 * g, 0] = k
    w = layers(rng, [0, 8, 9, 10, 11, 12, 13, 14, 15])
    change = np.array([0.0, -1, -2, 1])[(rng.permutation(N)[:, None] + 2 * (a // 4)) % 4]
    for g in range(8): w[:, g, 11, 0, g, 11, 0] = (4 * change[:, g]).astype(np.float32).astype(BF)
    return {**tiles(x, h, u.astype(BF), d["v"]), **weights(rng, w)}
def setup_inputs_ends(rng):
    d = numbers_of(rng)
    x, h = d["x"].astype(np.float32).reshape(N, 8, 16, C, 4), d["h"].astype(np.float32).reshape(N, 8, 16, B, 4)
    for t, s in ((x, np.argsort(rng.random((N, 8, C)), axis=2)), (h, rng.integers(0, C, (N, 8, B)))):
        z = ((s[..., None] >> np.arange(12)) & 1) * np.exp2(np.arange(12.0))
        t[:, :, 0] = 0
        for i in range(3): t[:, :, 8 + i] = z[..., 4 * i:4 * i + 4]
    k = np.stack([rng.permutation(8) for r in range(N)])
    x[:, :, 0, :, 0] = ((rng.permutation(8) < 2) * 512.0 * (np.arange(N) % 2)[:, None])[:, :, None]
    h[:, :, 0, :, 0] = np.array([-1024.0, -1024, 1024, 1024, 0, 0, 0, 0])[k][:, :, None]
    x[:, :, 4] = 0
    x[:, :, 4, :, 0] = 64
    w = layers(rng, [0, 8, 9, 10, 11, 12, 13, 14, 15])
    for g in range(8): w[:, g, 4, 0, g, 0, 0] = np.array([1024.0, 0, -1024, 0, 1024, -1024, 0, 0])[k[:, g]].astype(np.float32).astype(BF)
    u = d["u"][0].astype(np.float32).reshape(128, 128, 4)
    u[:, ::16] = 0
    for g in range(8):
        u[16 * g, 16 * g, 0] = 1
        u[16 * g + 8:16 * g + 11, 16 * g] = 1
    return {**tiles(x, h, u.astype(BF), d["v"]), **weights(rng, w)}
def setup_inputs_huge(rng):
    d = numbers_of(rng)
    k = rng.permutation(8)
    def sized(n):
        s = np.where((k < 4)[:, None, None, None], rng.choice([-1.0, 1.0], (N, 8, 1, n, 1)), 1.0)
        return ((0.7 + 0.2 * rng.random((N, 8, 1, n, 1))) * (0.95 + 0.05 * rng.random((N, 8, 16, n, 4))) * s * 2.0 ** 30).astype(np.float32)
    u = d["u"][0].astype(np.float32).reshape(8, 16, 8, 16, 4)
    u[:, :, :, 0] = 2.0 ** 30 * (1 - 0.1 * rng.random((8, 16, 8, 4))) * (k % 2 * 2.0 - 1.0)[:, None]
    w = np.zeros((N, 128, 4, 128, 4), np.float32)
    i = np.arange(128)
    for b in range(4): w[:, i, b, i, b] = -1
    return {**tiles(sized(C), sized(B), u.astype(BF), d["v"]), **weights(rng, w.astype(BF))}
def setup_inputs_spread(rng):
    d = setup_inputs(rng)
    d["x"] = big(wide(rng, N, 128, 4 * C, cols=6))
    d["h"] = wide(rng, N, 128, 4 * B)
    return d
def check_inputs(d):
    b = []
    for k in ("x", "h", "u", "v"):
        a = np.abs(d[k].astype(np.float32))
        if not (np.isfinite(a).all() and ((a == 0) | (a >= 2.0 ** -30) & (a <= 2.0 ** 30)).all()): b.append("a value of " + k)
    a = d["u"].astype(np.float32)
    if (a != a[:1]).any(): b.append("u: not the same on all ranks")
    a = a.reshape(N, 8, 16, 8, 16, 4)
    for g in range(8):
        if (a[:, np.arange(8) != g, :, g, 0] != 0).any(): b.append("u: column 16 * g outside group g")
    none, least, most = [emit(mx_ref.quantize(np.full((128, 16), k, np.float32).astype(BF)))[1][0, 0] for k in (0.0, 2.0 ** -30, 2.0 ** 30)]
    for r in range(N):
        if ((d["wc"][r] == 0x7F) | (d["wc"][r] == 0xFF)).any(): b.append("wc: a code that is no number")
        s = mx_ref.live(d["ws"][r])
        if ((s != none) & ((s < least) | (s > most))).any(): b.append("ws: a scale out of range")
    return b
def keys(qu, c):
    return mx_ref.matmul(qu, c)[::16] + np.float32(0.0)
def order(k):
    return np.argsort(k, axis=1, kind="stable")
def step(t, m, p, a, w):
    lower = gcols(t, np.take_along_axis(m, np.maximum(p - 1, 0), axis=1)).astype(np.float32)
    upper = gcols(t, np.take_along_axis(m, np.minimum(p, m.shape[1] - 1), axis=1)).astype(np.float32)
    z = mx_ref.quantize(((lower + upper) * np.float32(0.5)).astype(BF))
    d = decode(a)
    return tile([mx_ref.matmul(pick(w, np.arange(128 * b, 128 * b + 128)), z) * np.float32(0.03125) + d[:, b::4] for b in range(4)])
def reference(x, h, u, v, wc, ws):
    qu = [mx_ref.quantize(u[r]) for r in range(N)]
    lay = [pk(wc[r], ws[r]) for r in range(N)]
    k0 = [keys(qu[r], mx_ref.quantize(x[r])) for r in range(N)]
    m0 = [order(k0[r]) for r in range(N)]
    sample = [mx_ref.quantize(gcols(x[r], m0[r][:, 1::2])) for r in range(N)]
    sent, bridge = [], []
    for r in range(N):
        came = sample[(r + 1) % N]
        k1 = np.concatenate([k0[r], keys(qu[r], came)], axis=1)
        a = mx_ref.quantize(h[r])
        below = k1[:, None, :] < keys(qu[r], a)[:, :, None]
        t = np.concatenate([x[r], decode(came).astype(BF)], axis=1)
        sent.append(mx_ref.quantize(step(t, order(k1), np.sum(below, axis=2), a, lay[r])))
        bridge.append(2 * np.sum(below[:, :, C:], axis=2))
    y, ov = np.zeros((N, 128, B), np.float32), np.zeros((N, 8, B), np.float32)
    oc, osc = np.zeros((N, 128, 4 * B), np.uint8), np.zeros((N, 16, B), np.uint8)
    for r in range(N):
        a, i = sent[r - 1], np.clip(bridge[r - 1], 1, C - 1)
        s, k = keys(qu[r], a), np.take_along_axis(k0[r], m0[r], axis=1)
        p = i + (s > np.take_along_axis(k, i, axis=1)) - (s < np.take_along_axis(k, i - 1, axis=1))
        last = mx_ref.quantize(step(x[r], m0[r], p, a, lay[r]))
        y[r] = mx_ref.matmul(mx_ref.quantize(v[r]), last)
        ov[r] = p
        oc[r], osc[r] = emit(last)
    return {"y": y, "ov": ov, "oc": oc, "osc": osc}

from concourse.bass import DstId, RemoteDMATransfer
from concourse.mybir import dt, AluOpType as A, ActivationFunctionType as F

C, B, S = 448, 192, 224
X4, U8, BF, F32, U16, I32 = "float8_e4m3fn_x4", "uint8", "bfloat16", "float32", "uint16", "int32"
BIG, BIG2, H = 2.0 ** 90, 2.0 ** 92, 2.0 ** 14
WID = [448, 384, 320, 256, 192, 128, 128]
OFF = [sum(WID[:q]) for q in range(7)]
SELF = [26, 22, 18]
JP, MP = 704, 464
PART = {"aa": ("sm", 0), "t2": ("sm", 24), "t3": ("sm", 48), "pp": ("sm", 72), "pt": ("sm", 96), "se1": ("sm", 120), "t1": ("sm", 128),
        "rq": ("sm", 160), "spo": ("sm", 192), "sps": ("sm", 224),
        "lo1": ("li", 0), "ls1": ("li", 16), "lb": ("li", 32), "sel": ("li", 48), "lo2": ("li", 64), "lu": ("li", 96)}


def slot(c):
    return (28 - c) // 4, (28 - c) % 4


SCRATCH = {}
for _n, _w, _d in [
    ("xs", 4 * C, BF), ("hs", 4 * B, BF), ("us", 512, BF), ("vs", 512, BF),
    ("qx", C, X4), ("sx", C, U8), ("qh", B, X4), ("sh", B, U8), ("qu0", 128, X4), ("su0", 128, U8),
    ("qu", 128, X4), ("su", 128, U8), ("qv", 128, X4), ("sv", 128, U8), ("qw", 512, X4), ("sw", 512, U8),
    ("rxq", C, X4), ("rxs", C, U8), ("rl", 16, U16), ("rb", 16, U16), ("ryq", B, X4), ("rys", B, U8),
    ("qx2", C, X4), ("sx2", C, U8), ("sl2", 16, U16), ("br2", 16, U16), ("qy2", B, X4), ("sy2", B, U8),
    ("pi", 16, I32), ("ul", 16, U16), ("col", 32, F32), ("rb16", 16, BF), ("cb", 32, F32),
    ("jm", C, BF), ("gi", 128, BF), ("i128", 128, BF), ("iot", MP, F32), ("z0", 512, BF), ("j32", 64, BF), ("tmp", 256, BF),
    ("nn", C, BF), ("m2", C, BF), ("mh", C, BF), ("d0", C, BF), ("d2", 2 * B, BF),
    ("wn", 512, BF), ("qwn", 128, X4), ("swn", 128, U8), ("wk", 512, BF), ("qwk", 128, X4), ("swk", 128, U8),
    ("et", 2048, BF), ("qe", 512, X4), ("se", 512, U8),
    ("ksb", C, F32), ("xm", C, F32), ("kx", C, F32), ("fl", 4 * sum(WID), BF), ("qf", sum(WID), X4), ("sf", sum(WID), U8),
    ("sg", C, BF), ("junk", 6048, BF), ("rw", 32, F32), ("sm", 240, F32), ("li", 128, U16), ("sc", C, F32), ("rk", 32, U16),
    ("mm", C, F32), ("scs", S, F32), ("sl", 16, U16), ("scm", C, F32), ("ml", 32, U16), ("ml4", 112, U16),
    ("ks", 464, F32), ("k2", C, F32), ("s1", B, F32), ("dh", 4 * C, BF), ("jt", 4 * JP, BF),
    ("fo", 4 * B, BF), ("qfo", B, X4), ("sfo", B, U8), ("wo", C, F32), ("sco", B, F32), ("sco2", B, F32), ("ko", 2 * B, F32),
    ("gs", 240, F32), ("fs", 4 * B, BF), ("qfs", B, X4), ("sfs", B, U8), ("wsm", S, F32),
    ("scx", B, F32), ("scx2", B, F32), ("la", 16, U16), ("ff", 2 * B, BF), ("scf", 2 * B, BF),
    ("lh", 4 * B, BF), ("zt", 4 * B, BF), ("qz", B, X4), ("sz", B, U8), ("yt", 4 * B, BF), ("qy", B, X4), ("sy", B, U8),
    ("mt", 4 * MP, BF), ("bw", 48, F32), ("lk", 32, U16), ("kk", 2 * B, F32), ("f2", 2 * B, BF), ("sc2", 2 * B, BF),
    ("t4", 16, F32), ("lp", 16, U16), ("pv", B, F32), ("zu", 4 * B, BF), ("qz2", B, X4), ("sz2", B, U8),
    ("yu", 4 * B, BF), ("qo", B, X4), ("so", B, U8), ("yo", B, F32),
]:
    SCRATCH[_n] = ("sbuf", [128, _w], _d)
for _b in range(8):
    SCRATCH["b%d" % _b] = ("psum", [128, 512], F32)

SEMAPHORES = ["cv", "ca", "cp", "cg", "du", "dx", "dy", "dh", "dv", "dw", "st", "ls", "ax", "al", "ab", "ay", "hx", "hl", "hb", "hy"]


def helpers(T, topo, rank):
    n = len(T.cores)
    me, before, nxt = T.cores[rank], T.cores[(rank - 1) % n], T.cores[(rank + 1) % n]
    ok = [c for c in topo.cores_of(me) if T.rank_of(c) is None and topo.may_write(c, before) and topo.may_write(c, nxt)]
    near = [c for c in ok if topo.die(c) == topo.die(me)]
    far = [c for c in ok if topo.die(c) != topo.die(me)]
    return near[0], far[0], near[1]


def write(g, T, topo, src, dst, out, in_, sem):
    rid, pid = topo.addr(dst, src)
    g.remote_dma(out, in_, T.sem[sem], T.sem.ls, pid, rid, topo.mask(src, dst))
    return len(topo.engines(src, dst))


def u8(v):
    return v.bitcast(dt.uint8)


def arrivals(T, topo, src_rank, dst, via, direct_calls):
    src = T.cores[src_rank]
    if direct_calls and topo.may_write(src, dst):
        return direct_calls * len(topo.engines(src, dst))
    return sum(len(topo.engines(h, dst)) for h in via)


def helper_program(g, core, T, topo, rank):
    n = len(T.cores)
    me, before, nxt = T.cores[rank], T.cores[(rank - 1) % n], T.cores[(rank + 1) % n]
    role = helpers(T, topo, rank).index(core)
    full = len(topo.engines(me, core))
    sent = 0
    if role < 2:
        a = role * (C // 2)
        g.wait_ge(T.sem.hx, full // 2)
        sent += write(g, T, topo, core, before, u8(T.qx2[:, a:a + C // 2]), u8(T.rxq[:, a:a + C // 2]), "ax")
    else:
        g.wait_ge(T.sem.hx, full)
        sent += write(g, T, topo, core, before, T.sx2[:], T.rxs[:], "ax")
    if role == 0 and not topo.may_write(me, before):
        g.wait_ge(T.sem.hl, full)
        sent += write(g, T, topo, core, before, T.sl2[:, 0:14], T.rl[:, 0:14], "al")
    if not topo.may_write(me, nxt):
        if role < 2:
            a = role * (B // 2)
            g.wait_ge(T.sem.hy, full // 2)
            sent += write(g, T, topo, core, nxt, u8(T.qy2[:, a:a + B // 2]), u8(T.ryq[:, a:a + B // 2]), "ay")
        else:
            g.wait_ge(T.sem.hb, full)
            sent += write(g, T, topo, core, nxt, T.br2[:, 0:12], T.rb[:, 0:12], "ab")
            g.wait_ge(T.sem.hy, full)
            sent += write(g, T, topo, core, nxt, T.sy2[:], T.rys[:], "ay")
    g.wait_ge(T.sem.ls, sent)


def rank_program(g, core, T, topo):
    rank = T.rank_of(core)
    n = len(T.cores)
    if rank is None:
        for r in range(n):
            if core in topo.cores_of(T.cores[r]) and core in helpers(T, topo, r):
                helper_program(g, core, T, topo, r)
        return
    before, nxt = T.cores[(rank - 1) % n], T.cores[(rank + 1) % n]
    ha, hb, hc = helpers(T, topo, rank)
    hn, hp = helpers(T, topo, (rank + 1) % n), helpers(T, topo, (rank - 1) % n)
    V, AC, PE = g.vector, g.scalar, g.tensor
    queue = {"v": V, "a": AC, "p": PE, "g": g, "s": g.sync}
    count = {"v": 0, "a": 0, "p": 0, "g": 0}
    seen = {q: {} for q in queue}
    wrote, readers, bank = {}, {}, {}
    sent, stores = [0], [0]
    wrote["x2"] = ("ax", arrivals(T, topo, (rank + 1) % n, core, hn, 0))
    wrote["sl2"] = ("al", arrivals(T, topo, (rank + 1) % n, core, hn[:1], 1))
    wrote["br2"] = ("ab", arrivals(T, topo, (rank - 1) % n, core, hp[2:], 1))
    wrote["y2"] = ("ay", arrivals(T, topo, (rank - 1) % n, core, hp, 2))

    def P(name, a, b):
        buf, o = PART[name]
        return T[buf][:, o + a:o + b]

    def need(q, tokens):
        most = {}
        for s, v in tokens:
            most[s] = max(most.get(s, 0), v)
        for s, v in most.items():
            if seen[q].get(s, 0) < v:
                queue[q].wait_ge(T.sem[s], v)
                seen[q][s] = v

    def order(q, r, w, b):
        t = [wrote[k] for k in r + w if k in wrote]
        for k in w:
            t += readers.get(k, [])
        for k in b:
            t += [v for qq, v in bank.get(k, {}).items() if qq != q]
        need(q, t)

    def op(q, fn, r="", w="", b=""):
        r, w, b = r.split(), w.split(), b.split()
        order(q, r, w, b)
        count[q] += 1
        fn().then_inc(T.sem["c" + q], 1)
        tok = ("c" + q, count[q])
        for k in r:
            readers.setdefault(k, []).append(tok)
        for k in w:
            wrote[k] = tok
            readers[k] = []
        for k in b:
            bank.setdefault(k, {})[q] = tok

    def load(q, out, in_, sem, w, total=16):
        queue[q].dma_start(out, in_).then_inc(T.sem[sem], 16)
        wrote[w] = (sem, total)

    def store(q, out, in_, r):
        order(q, r.split(), [], [])
        queue[q].dma_start(out, in_).then_inc(T.sem.st, 16)
        stores[0] += 16

    def ts(out, in0, s1, s2, o0, o1=None, r="", w="", b=""):
        if o1 is None:
            op("v", lambda: V.tensor_scalar(out, in0, s1, None, o0), r, w, b)
        else:
            op("v", lambda: V.tensor_scalar(out, in0, s1, s2, o0, o1), r, w, b)

    def tt(out, a, c, o, r="", w="", b=""):
        op("v", lambda: V.tensor_tensor(out, a, c, o), r, w, b)

    def scan(out, d0, d1, o0, o1, r="", w="", b="", init=0.0):
        op("v", lambda: V.tensor_tensor_scan(out, d0, d1, init, o0, o1), r, w, b)

    def cp(out, in_, r="", w="", b=""):
        op("v", lambda: V.tensor_copy(out, in_), r, w, b)

    def quant(q, s, t, r, w):
        op("v", lambda: V.quantize_mx(q, s, t), r, w)

    def act(out, in_, r="", w="", b="", f=F.Identity, **kw):
        op("a", lambda: AC.activation(out, in_, f, **kw), r, w, b)

    def mx(bk, cols, lq, ls, rq, rs, r, start=True, stop=True):
        op("p", lambda: PE.matmul_mx(T[bk][:, 0:cols], lq, ls, rq, rs, start, stop), r, "", bk)

    def unpack(cols, q, s, r, stop):
        for b in range(4):
            mx("b%d" % (4 + b), cols, T.qe[:, 128 * b:128 * b + 128], T.se[:, 128 * b:128 * b + 128], q, s, r, True, stop)

    def iota(out, pat, cm, w, flag=True):
        if flag:
            op("g", lambda: g.iota(out, pat, 0, cm, allow_small_or_imprecise_dtypes=True), "", w)
        else:
            op("g", lambda: g.iota(out, pat, 0, cm), "", w)

    def halves(land, src, half, sem):
        moves = []
        for i, h in enumerate((ha, hb)):
            e = topo.engines(core, h)
            e = e[i * len(e) // 2:(i + 1) * len(e) // 2]
            rid, pid = topo.addr(h, core)
            moves.append(RemoteDMATransfer(dst_ids=[DstId(rid=rid, pnc=pid)], dma_engine_mask=sum(1 << k for k in e), remote_sem=T.sem[sem],
                                           src=u8(src[:, i * half:(i + 1) * half]), dst=u8(land[:, i * half:(i + 1) * half])))
            sent[0] += len(e)
        g.remote_dma_fused(moves, local_sem=T.sem.ls)

    def col(k):
        return T.col[:, k:k + 1]
    R, GP, PF, INV, INVH, HH, SP, NSP, H32, RC, C479, C480, C31, C32, THR, C465, W1, W2, BP, R1, R2, R3 = range(22)

    load("a", T.us[:], T.u[:], "du", "us")
    load("s", T.xs[:, 0:2 * C], T.x[:, 0:2 * C], "dx", "xa")
    load("s", T.xs[:, 2 * C:], T.x[:, 2 * C:], "dy", "xb")
    load("s", T.hs[:], T.h[:], "dh", "hs")
    load("s", u8(T.qw[:]), T.wc[:], "dw", "w", 32)
    load("s", T.sw[:], T.ws[:], "dw", "w", 32)
    load("s", T.vs[:], T.v[:], "dv", "vs")

    iota(T.pi[:, 0:1], [[0, 1]], 1, "pi", flag=False)
    iota(T.pi[:, 8:16], [[16, 8]], 0, "ui", flag=False)
    iota(T.jm[:], [[0, 28], [1, 16]], 0, "jm")
    iota(T.gi[:], [[1, 8], [0, 16]], 0, "gi")
    iota(T.i128[:], [[1, 128]], 0, "i128")
    iota(col(PF), [[0, 1]], 1, "cP")
    iota(T.cb[:, 0:28], [[-16, 28]], 0, "cb0")
    iota(T.iot[:], [[1, MP]], 0, "iot")
    iota(T.j32[:], [[0, 2], [1, 32]], 0, "j32")
    op("v", lambda: V.memset(T.z0[:], 0.0), "", "z0")
    ts(T.pi[:, 2:3], T.pi[:, 0:1], 15, None, A.bitwise_and, r="pi", w="pr")
    ts(T.pi[:, 4:5], T.pi[:, 0:1], 4, None, A.arith_shift_right, r="pi", w="pg")
    cp(T.ul[:, 0:8], T.pi[:, 8:16], "ui", "ul")
    cp(col(R), T.pi[:, 2:3], "pr", "cR")
    cp(T.rb16[:, 0:1], T.pi[:, 2:3], "pr", "r0")
    cp(col(GP), T.pi[:, 4:5], "pg", "cG")
    ts(col(INV), col(R), 15.0, 1.0 / H, A.is_ge, A.max, r="cR", w="cI")
    ts(col(INVH), col(R), 15.0, 1.0 / H, A.is_lt, A.max, r="cR", w="cJ")
    ts(col(W1), col(R), 11.0, -8192.0, A.is_lt, A.mult, r="cR", w="cW1")
    ts(col(W2), col(R), 13.0, -8192.0, A.is_lt, A.mult, r="cR", w="cW2")
    ts(col(R1), col(R), 1.0, None, A.add, r="cR", w="r1")
    rb0 = T.rb16[:, 0:1]
    ts(T.nn[:], T.jm[:], rb0, -BIG, A.not_equal, A.mult, r="jm r0", w="nn")
    ts(T.m2[:], T.jm[:], rb0, -BIG, A.is_le, A.mult, r="jm r0", w="m2")
    ts(T.tmp[:, 0:64], T.jm[:, 0:64], rb0, None, A.is_gt, r="jm r0", w="ta")
    ts(T.tmp[:, 64:128], T.jm[:, 0:64], col(R1), H, A.is_equal, A.mult, r="jm r1", w="tb")
    ts(T.mh[:], T.jm[:], rb0, BIG, A.is_equal, A.mult, r="jm r0", w="mh")
    tt(T.d0[:, 0:64], T.tmp[:, 0:64], T.tmp[:, 64:128], A.max, "ta tb", "d0a")
    for t in range(4):
        ts(T.wn[:, t::4], T.gi[:], col(GP), -2.0 ** -9, A.is_equal, A.mult, r="gi cG", w="wn%d" % t)
    quant(T.qu0[:], T.su0[:], T.us[:], "us", "qu0")
    quant(T.qwn[:], T.swn[:], T.wn[:], "wn0 wn1 wn2 wn3", "qwn")
    cp(T.qu[:].bitcast(dt.uint32), T.qu0[:].bitcast(dt.uint32).indirect(T.ul[:, 0:8]), "qu0 ul", "qu")
    cp(T.su[:], T.su0[:].indirect(T.ul[:, 0:8]), "qu0 ul", "su")
    for b in range(4):
        act(T.et[:, 512 * b:512 * b + 512], T.z0[:], "z0", "ez%d" % b)
    act(col(SP), col(INVH), "cJ", "cS", scale=32.0)
    act(col(NSP), col(INVH), "cJ", "cN", scale=-32.0)
    act(T.d0[:, 64:128], T.d0[:, 0:64], "d0a", "d0b")
    for q in range(7):
        lo = 16 * (25 - 4 * q)
        act(T.fl[:, 4 * (OFF[q] + lo):4 * (OFF[q] + WID[q])], T.z0[:, 0:4 * (WID[q] - lo)], "z0", "zz%d" % q)
        if q == 0:
            act(T.d0[:, 128:256], T.d0[:, 0:128], "d0a d0b", "d0c")
        if q == 1:
            act(T.d0[:, 256:448], T.d0[:, 0:192], "d0a d0b d0c", "d0")
    act(T.rw[:, 0:1], T.z0[:, 0:1], "z0", "rw0")
    act(T.cb[:, 0:28], T.cb[:, 0:28], "cS", "cb0", scale=col(SP))
    act(col(H32), col(INV), "cI", "cH32", scale=H / 32)
    act(col(RC), col(R), "cR", "cRC", bias=432.45)
    act(col(R2), col(R), "cR", "r2", scale=2.0)
    act(col(R3), col(R1), "r1", "r3", scale=2.0)
    for b in range(4):
        ts(T.et[:, 513 * b:512 * b + 512:4], T.i128[:], col(PF), 32.0, A.is_equal, A.mult, r="i128 cP ez%d" % b, w="e%d" % b)
    quant(T.qe[:], T.se[:], T.et[:], "e0 e1 e2 e3", "qe")

    quant(T.qx[:, 0:C // 2], T.sx[:, 0:C // 2], T.xs[:, 0:2 * C], "xa", "qxa")
    quant(T.qx[:, C // 2:], T.sx[:, C // 2:], T.xs[:, 2 * C:], "xb", "qxb")
    mx("b0", C, T.qu[:], T.su[:], T.qx[:], T.sx[:], "qu su qxa qxb")
    mx("b1", C, T.qu[:], T.su[:], T.qx[:], T.sx[:], "qu su qxa qxb")
    order("g", ["qxa", "qxb"], [], [])
    halves(T.rxq, T.qx, C // 2, "hx")
    sent[0] += write(g, T, topo, core, hc, T.rxs[:], T.sx[:], "hx")
    act(T.ksb[:], T.b1[:, 0:C], "", "ksb", "b1")
    for t, k in enumerate((-8192.0, col(W1), col(W2), -512.0)):
        act(T.wk[:, t::4], T.wn[:, 0::4], "wn0 cW1 cW2", "wk%d" % t, scale=k)
    K = T.b0
    ts(T.tmp[:, 128:192], T.j32[:], col(R2), None, A.is_gt, r="j32 r2", w="tc")
    ts(T.tmp[:, 192:256], T.j32[:], col(R3), H, A.is_equal, A.mult, r="j32 r3", w="td")
    tt(T.xm[:], K[:, 0:C], T.nn[:], A.add, "nn", "xm", "b0")
    scan(T.kx[:], T.m2[:], T.xm[:], A.add, A.max, "m2 xm", "kx", init=-BIG)

    def flags(c):
        q, t = slot(c)
        return T.fl[:, 4 * OFF[q] + t:4 * (OFF[q] + 16 * c):4]

    def kcol(c):
        return T.kx[:, 16 * c + 15:16 * c + 16]

    def sign1(c):
        act(T.sg[:, 0:16 * c], T.ksb[:, 0:16 * c], "ksb kx", "sg", f=F.Sign, bias=kcol(c), scale=-1.0)

    def sign2(c):
        act(flags(c), T.sg[:, 0:16 * c], "sg zz%d" % slot(c)[0], "f%d rq%d" % (c, c), f=F.Sign, bias=1.0, accum_out=P("rq", c, c + 1))

    def row(c):
        act(T.junk[:, 8 * c * (c - 1):8 * c * (c + 1)], flags(c), "f%d cS cN" % c, "rw%d" % c, bias=col(NSP), scale=col(SP), accum_out=T.rw[:, c:c + 1])

    def tile_done(q):
        a, w = OFF[q], WID[q]
        cs = [c for c in range(1, 28) if slot(c)[0] == q]
        quant(T.qf[:, a:a + w], T.sf[:, a:a + w], T.fl[:, 4 * a:4 * (a + w)], " ".join("f%d" % c for c in cs) + (" df" if q == 0 else ""), "qf%d" % q)
        mx("b2", w, T.qwn[:], T.swn[:], T.qf[:, a:a + w], T.sf[:, a:a + w], "qwn qf%d" % q, q == 0, q == 6)
        if q == 0:
            mx("b2", w, T.qe[:, 0:128], T.se[:, 0:128], T.qf[:, 0:w], T.sf[:, 0:w], "qe qf0", False, False)

    sign1(SELF[0])
    tt(T.fl[:, 0:4 * C:4], K[:, 0:C], T.kx[:], A.is_lt, "kx zz0", "df", "b0")
    sign2(SELF[0])
    for q in range(7):
        cs = [c for c in range(27, 0, -1) if slot(c)[0] == q]
        later = [c for c in SELF if slot(c)[0] == q + 1]
        mine = [c for c in cs if c not in SELF]
        for i, c in enumerate(mine):
            ts(flags(c), K[:, 0:16 * c], kcol(c), None, A.is_le, r="kx zz%d" % q, w="f%d" % c, b="b0")
            if i == 0 and q > 0:
                tile_done(q - 1)
            if i == 0 and later:
                sign1(later[0])
            row(c)
            if i == 0 and later:
                sign2(later[0])
        for c in cs:
            if c in SELF:
                act(T.rw[:, c:c + 1], P("rq", c, c + 1), "rq%d cS cb0" % c, "rw%d" % c, bias=T.cb[:, c:c + 1], scale=col(SP))
    tile_done(6)
    quant(T.qh[:], T.sh[:], T.hs[:], "hs", "qh")
    mx("b3", B, T.qu[:], T.su[:], T.qh[:], T.sh[:], "qh")
    act(T.fo[:, 0:384], T.z0[:, 0:384], "z0", "fo0")
    act(T.fo[:, 384:768], T.z0[:, 0:384], "z0", "fo1")
    act(T.s1[:], T.b3[:, 0:B], "", "s1", "b3")
    act(T.fs[:, 0:384], T.z0[:, 0:384], "z0", "fs0")
    act(T.fs[:, 384:768], T.z0[:, 0:384], "z0", "fs1")
    for ap, v, nm in ((T.ks[:, 0:1], -BIG, "ksa"), (T.ks[:, C + 1:], BIG, "ksz"), (T.gs[:, 0:1], -BIG2, "gsa"), (T.gs[:, S + 1:], BIG2, "gsb")):
        act(ap, T.z0[:, 0:1 if v < 0 else 15], "z0", nm, bias=v)
    act(col(HH), col(INV), "cI", "cH", scale=H)
    act(col(BP), col(INVH), "cJ", "cB", scale=H)
    for k, v in ((C479, 479.0), (C480, 480.0), (C31, 31.0), (C32, 32.0), (THR, 447.7 * H), (C465, 465.0)):
        act(col(k), col(INVH), "cJ", "c%d" % k, scale=v)
    mx("b1", C, T.qu[:], T.su[:], T.qx2[:], T.sx2[:], "x2")
    unpack(C, T.qx2[:], T.sx2[:], "qe x2", True)
    act(T.k2[:], T.b1[:, 0:C], "", "k2", "b1")
    for b in range(4):
        act(T.dh[:, C * b:C * b + C], T["b%d" % (4 + b)][:, 0:C], "", "dh%d" % b, "b%d" % (4 + b), scale=1.0 / 64)

    scan(T.sc[:], T.d0[:], T.b2[:, 0:C], A.mult, A.add, "d0", "sc", "b2")
    tt(P("t1", 0, 28), T.sc[:, 15::16], T.rw[:, 0:28], A.add, "sc " + " ".join("rw%d" % c for c in range(28)), "t1")
    ts(T.rk[:, 0:28], P("t1", 0, 28), col(H32), col(RC), A.mult, A.add, r="t1 cH32 cRC", w="rk")
    cp(T.mm[:].indirect(T.rk[:, 0:28]), T.iot[:, 0:C], "iot rk", "mm")
    scan(T.scs[:], T.d0[:, 0:S], T.mm[:, 1::2], A.mult, A.add, "mm", "scs")
    ts(T.sl[:, 0:14], T.scs[:, 15::16], col(INV), None, A.mult, r="scs cI", w="sl")
    order("g", ["sl"], [], [])
    if topo.may_write(core, before):
        sent[0] += write(g, T, topo, core, before, T.sl2[:, 0:14], T.sl[:, 0:14], "al")
    else:
        sent[0] += write(g, T, topo, core, ha, T.rl[:, 0:14], T.sl[:, 0:14], "hl")

    scan(T.scm[:], T.d0[:], T.mm[:], A.mult, A.add, "mm", "scm")
    quant(T.qwk[:], T.swk[:], T.wk[:], "wk0 wk1 wk2 wk3", "qwk")
    ts(T.ml[:, 0:28], T.scm[:, 15::16], col(INV), None, A.mult, r="scm cI", w="ml")
    cp(T.ks[:, 1:C + 1], T.ksb[:].indirect(T.ml[:, 0:28]), "ksb ml", "ks")
    scan(P("spo", 0, 28), T.mh[:, 0:28], T.ks[:, 16:C + 1:16], A.add, A.min, "mh ks", "spo")
    ts(T.fo[:, 0::4], T.s1[:], P("spo", 15, 16), None, A.is_gt, r="s1 spo fo0 fo1", w="foa")
    ts(T.fo[:, 1::4], T.s1[:], P("spo", 27, 28), None, A.is_gt, r="s1 spo fo0 fo1", w="fob")
    quant(T.qfo[:], T.sfo[:], T.fo[:], "foa fob foc", "qfo")
    mx("b0", B, T.qwk[:], T.swk[:], T.qfo[:], T.sfo[:], "qwk qfo")
    for t in range(4):
        ts(T.ml4[:, 28 * t:28 * t + 28], T.ml[:, 0:28], 4.0, float(t), A.mult, A.add, r="ml", w="ml4%d" % t)
        act(T.jt[:, JP * t + 32:JP * t + 32 + C], T.xs[:].indirect(T.ml4[:, 28 * t:28 * t + 28]), "xa xb ml4%d" % t, "jo%d" % t, scale=0.5)
    scan(T.sco[:], T.d0[:, 0:B], T.b0[:, 0:B], A.mult, A.add, "", "sco", "b0")
    scan(T.wo[:], T.mh[:], T.ks[:, 1:C + 1], A.add, A.min, "mh ks", "wo")
    ts(P("lo1", 0, 12), T.sco[:, 15::16], col(INV), 15.0, A.mult, A.add, r="sco", w="lo1")
    tt(T.fo[:, 3::4], T.wo[:].indirect(P("lo1", 0, 12)), T.s1[:], A.is_lt, "wo lo1", "foc")
    quant(T.qfo[:], T.sfo[:], T.fo[:], "foc", "qfo")
    mx("b0", B, T.qwk[:], T.swk[:], T.qfo[:], T.sfo[:], "qfo")
    unpack(B, T.qh[:], T.sh[:], "qe qh", False)
    tt(T.d2[:, 0:64], T.tmp[:, 128:192], T.tmp[:, 192:256], A.max, "tc td", "d2a")
    scan(T.sco2[:], T.d0[:, 0:B], T.b0[:, 0:B], A.mult, A.add, "", "sco2", "b0")
    cp(T.gs[:, 1:S + 1], T.k2[:].indirect(T.sl2[:, 0:14]), "k2 sl2", "gs")
    p0 = T.sco2[:, 15::16]
    ts(P("lo2", 0, 12), p0, col(INV), None, A.mult, r="sco2", w="lo2a")
    ts(P("lo2", 12, 24), p0, col(INV), 1.0, A.mult, A.add, r="sco2", w="lo2b")
    act(T.ko[:], T.ks[:].indirect(P("lo2", 0, 24)), "ks ksa ksz lo2a lo2b", "ko")

    for t in range(4):
        act(T.jt[:, JP * t + 32 + C:JP * t + JP], T.dh[:, C * t:C * t + C].indirect(T.sl2[:, 0:14]), "dh%d sl2" % t, "js%d" % t)
    scan(P("sps", 0, 14), T.mh[:, 0:14], T.gs[:, 16:S + 1:16], A.add, A.min, "gs", "sps")
    ts(P("pt", 0, 12), p0, 1.0 / H, col(C32), A.mult, A.add, r="sco2 c%d" % C32, w="pta")
    ts(T.fs[:, 2::4], T.s1[:], P("sps", 13, 14), None, A.is_gt, r="sps fs0 fs1", w="fsa")
    ts(P("pt", 12, 24), p0, col(THR), col(C465), A.is_ge, A.mult, r="sco2 c%d c%d" % (THR, C465), w="ptb")
    quant(T.qfs[:], T.sfs[:], T.fs[:], "fsa fsc", "qfs")
    mx("b0", B, T.qwk[:], T.swk[:], T.qfs[:], T.sfs[:], "qfs")
    scan(T.wsm[:], T.mh[:, 0:S], T.gs[:, 1:S + 1], A.add, A.min, "gs", "wsm")
    ts(P("se1", 0, 1), T.gs[:, S:S + 1], T.ks[:, C:C + 1], float(S), A.is_ge, A.mult, r="gs", w="se1")
    ts(P("sel", 1, 2), T.gs[:, 1:2], T.ks[:, 1:2], float(C), A.is_lt, A.mult, r="gs", w="selb")
    scan(T.scx[:], T.d0[:, 0:B], T.b0[:, 0:B], A.mult, A.add, "", "scx", "b0")
    ts(P("sel", 0, 1), P("se1", 0, 1), float(C - 1), None, A.add, r="se1", w="sela")
    ts(P("ls1", 0, 12), T.scx[:, 15::16], col(INV), 15.0, A.mult, A.add, r="scx", w="ls1")
    tt(T.fs[:, 3::4], T.wsm[:].indirect(P("ls1", 0, 12)), T.s1[:], A.is_lt, "wsm ls1", "fsc")
    for t in range(4):
        act(T.jt[:, JP * t:JP * t + 32], T.jt[:, JP * t + 32:JP * t + JP].indirect(P("sel", 0, 2)), "sela selb jo%d js%d" % (t, t), "je%d" % t)
    act(T.d2[:, 64:128], T.d2[:, 0:64], "d2a", "d2b")
    act(T.mt[:, 0::MP], T.jt[:, 32::JP], "jo0 jo1 jo2 jo3", "mta", scale=2.0)
    act(T.d2[:, 128:256], T.d2[:, 0:128], "d2a d2b", "d2c")
    act(T.mt[:, C::MP], T.jt[:, 32 + C - 1::JP], "jo0 jo1 jo2 jo3", "mtb", scale=2.0)
    act(T.d2[:, 256:384], T.d2[:, 0:128], "d2a d2b", "d2d")
    quant(T.qfs[:], T.sfs[:], T.fs[:], "fsc", "qfs")
    mx("b0", B, T.qwk[:], T.swk[:], T.qfs[:], T.sfs[:], "qfs")
    ts(P("pp", 0, 12), p0, 1.0 / H, col(C31), A.mult, A.add, r="sco2 c%d" % C31, w="ppa")
    tt(P("pp", 12, 24), P("pt", 0, 12), P("pt", 12, 24), A.subtract, "pta ptb", "ppb")
    quant(T.qv[:], T.sv[:], T.vs[:], "vs", "qv")
    scan(T.scx2[:], T.d0[:, 0:B], T.b0[:, 0:B], A.mult, A.add, "", "scx2", "b0")
    a0 = T.scx2[:, 15::16]
    ts(T.la[:, 0:12], a0, col(INV), None, A.mult, r="scx2", w="la")
    ts(P("lb", 0, 12), a0, col(INV), 1.0, A.mult, A.add, r="scx2", w="lb")
    order("g", ["la"], [], [])
    if topo.may_write(core, nxt):
        sent[0] += write(g, T, topo, core, nxt, T.br2[:, 0:12], T.la[:, 0:12], "ab")
    else:
        sent[0] += write(g, T, topo, core, hc, T.rb[:, 0:12], T.la[:, 0:12], "hb")
    tt(T.ff[:, 0:B], T.gs[:].indirect(T.la[:, 0:12]), T.ko[:, 0:B], A.is_ge, "la ko gsa gsb", "ffa")
    tt(T.ff[:, B:2 * B], T.gs[:].indirect(P("lb", 0, 12)), T.ko[:, B:2 * B], A.is_lt, "lb ko", "ffb")
    ts(P("aa", 0, 12), a0, 1.0 / H, col(C479), A.mult, A.add, r="scx2 c%d" % C479, w="aaa")
    ts(P("aa", 12, 24), a0, 1.0 / H, col(C480), A.mult, A.add, r="scx2 c%d" % C480, w="aab")
    scan(T.scf[:], T.d0[:, 0:2 * B], T.ff[:], A.mult, A.add, "ffa ffb", "scf")
    tt(P("t2", 0, 24), T.scf[:, 15::16], P("aa", 0, 24), A.min, "scf aaa aab", "t2")
    tt(P("t3", 0, 24), P("t2", 0, 24), P("pp", 0, 24), A.max, "t2 ppa ppb", "t3")
    ts(P("lu", 0, 24), P("t3", 0, 24), col(HH), None, A.mult, r="t3 cH", w="lu")
    for t in range(4):
        win = T.jt[:, JP * t:JP * t + JP]
        act(T.lh[:, B * t:B * t + B], win.indirect(P("lu", 0, 12)), "lu je%d" % t, "lh%d" % t)
        tt(T.zt[:, t::4], win.indirect(P("lu", 12, 24)), T.lh[:, B * t:B * t + B], A.add, "lu je%d lh%d" % (t, t), "zt%d" % t)

    def layer(z, qz, sz, y, qy, sy, tag):
        quant(qz[:], sz[:], z[:], " ".join("%s%d" % (tag, t) for t in range(4)), tag + "q")
        for b in range(4):
            bk = "b%d" % (4 + b)
            mx(bk, B, T.qw[:, 128 * b:128 * b + 128], T.sw[:, 128 * b:128 * b + 128], qz[:], sz[:], "w " + tag + "q", False, True)
            if b % 2 == 0:
                act(y[:, b::4], T[bk][:, 0:B], "", "%sy%d" % (tag, b), bk, scale=0.03125)
            else:
                ts(y[:, b::4], T[bk][:, 0:B], 0.03125, None, A.mult, w="%sy%d" % (tag, b), b=bk)
        quant(qy[:], sy[:], y[:], " ".join("%sy%d" % (tag, b) for b in range(4)), tag + "Q")

    layer(T.zt, T.qz, T.sz, T.yt, T.qy, T.sy, "zt")
    order("g", ["ztQ"], [], [])
    if topo.may_write(core, nxt):
        sent[0] += write(g, T, topo, core, nxt, u8(T.qy2[:]), u8(T.qy[:]), "ay")
        sent[0] += write(g, T, topo, core, nxt, T.sy2[:], T.sy[:], "ay")
    else:
        halves(T.ryq, T.qy, B // 2, "hy")
        sent[0] += write(g, T, topo, core, hc, T.rys[:], T.sy[:], "hy")

    for t in range(4):
        a = JP * t + 32
        tt(T.mt[:, MP * t + 1:MP * t + C], T.jt[:, a:a + C - 1], T.jt[:, a + 1:a + C], A.add, "jo%d" % t, "mt%d" % t)
        if t == 0:
            ts(T.bw[:, 0:12], T.br2[:, 0:12], 2.0, 1.0, A.mult, A.max, r="br2", w="bwa")
        if t == 1:
            ts(T.lk[:, 0:12], T.bw[:, 0:12], float(C - 1), None, A.min, r="bwa", w="lka")
            ts(T.lk[:, 12:24], T.bw[:, 0:12], float(C - 1), 1.0, A.min, A.add, r="bwa", w="lkb")
            ts(T.bw[:, 16:28], T.bw[:, 0:12], float(C - 1), -1.0, A.min, A.add, r="bwa", w="bwb")
            act(T.kk[:], T.ks[:].indirect(T.lk[:, 0:24]), "lka lkb", "kk")
        if t == 2:
            ts(T.bw[:, 32:44], T.bw[:, 16:28], col(BP), None, A.mult, r="bwb cB", w="bwc")

    mx("b1", B, T.qu[:], T.su[:], T.qy2[:], T.sy2[:], "y2")
    unpack(B, T.qy2[:], T.sy2[:], "y2", False)
    tt(T.f2[:, 0::2], T.b1[:, 0:B], T.kk[:, 0:B], A.is_ge, "kk", "f2a", "b1")
    tt(T.f2[:, 1::2], T.b1[:, 0:B], T.kk[:, B:2 * B], A.is_gt, "kk", "f2b", "b1")
    scan(T.sc2[:], T.d2[:], T.f2[:], A.mult, A.add, "f2a f2b d2a d2b d2c d2d", "sc2")
    tt(T.t4[:, 0:12], T.sc2[:, 31::32], T.bw[:, 32:44], A.add, "sc2 bwc", "t4")
    ts(T.lp[:, 0:12], T.t4[:, 0:12], col(INV), 0.25, A.mult, A.add, r="t4", w="lp")
    for t in range(4):
        win = T.mt[:, MP * t:MP * t + C + 1]
        if t % 2 == 0:
            act(T.zu[:, t::4], win.indirect(T.lp[:, 0:12]), "lp mta mtb mt%d" % t, "zu%d" % t)
        else:
            cp(T.zu[:, t::4], win.indirect(T.lp[:, 0:12]), "lp mta mtb mt%d" % t, "zu%d" % t)
    act(T.pv[:], T.iot[:].indirect(T.lp[:, 0:12]), "lp", "pv")
    store("s", T.ov[:], T.pv[0:128:16, :], "pv")
    layer(T.zu, T.qz2, T.sz2, T.yu, T.qo, T.so, "zu")
    mx("b3", B, T.qv[:], T.sv[:], T.qo[:], T.so[:], "qv zuQ")
    store("s", T.oc[:], u8(T.qo[:]), "zuQ")
    for k in range(4):
        store("s", T.osc[4 * k:4 * k + 4, :], T.so[32 * k:32 * k + 4, :], "zuQ")
    act(T.yo[:], T.b3[:, 0:B], "", "yo", "b3")
    store("a", T.y[:], T.yo[:], "yo")
    need("g", [("c" + q, count[q]) for q in count] + [("ls", sent[0]), ("st", stores[0])])
